import numpy as np
import ml_dtypes


def mxq(x, axis, fmt="e4m3"):
    dtype, down = {"e4m3": (ml_dtypes.float8_e4m3fn, 7), "e5m2": (ml_dtypes.float8_e5m2, 14)}[fmt]
    v = np.moveaxis(np.asarray(x, np.float32).astype(ml_dtypes.bfloat16).astype(np.float64), axis, -1)
    blocks = v.reshape(v.shape[:-1] + (-1, 32))
    amax = np.abs(blocks).max(-1, keepdims=True)
    byte = np.maximum(np.where(amax > 0, np.frexp(amax)[1] - 1 + 127, 0) - down, 1)
    scale = np.exp2(byte - 127.0)
    codes = (blocks / scale).astype(np.float32).astype(dtype).astype(np.float64)
    return np.moveaxis((codes * scale).reshape(v.shape), -1, axis)


WIDE = False


def mx_kscale(k):
    if not WIDE:
        return np.ones(k)
    levels = np.array([10, -10, 5, -5, 0])
    if k % 512:
        return np.exp2(np.random.permutation(np.resize(levels, k // 32))).repeat(32)
    a = np.empty((k // 512, 16))
    for p in range(k // 512):
        a[p, :8] = np.random.permutation(np.resize(levels, 8))
        for g in range(8):
            far = levels[np.abs(levels - a[p, g]) >= 10]
            a[p, g + 8] = far[np.random.randint(len(far))]
    return np.exp2(a.ravel()).repeat(32)


def f64(x):
    return np.asarray(x).astype(np.float64)


def striped(idx):
    return np.tile(idx.reshape(-1, 16).T, (8, 1)).astype(np.uint16)


def unstriped(offs):
    return offs[:16].T.reshape(-1).astype(np.int64)


def striped8(idx):
    return np.concatenate([x.reshape(-1, 16).T for x in idx]).astype(np.uint16)


def runs(offs, k):
    lists = np.stack([offs[16 * r : 16 * r + 16].T.reshape(-1) for r in range(8)]).astype(np.int64)
    return lists[np.arange(k) % 512 // 64]


def pack_weight(w):
    k, n = w.shape
    w = f64(np.asarray(w, np.float32).astype(ml_dtypes.bfloat16)).reshape(k // 32, 32, n)
    amax = np.abs(w).max(1)
    byte = np.clip(np.where(amax > 0, np.frexp(amax)[1] - 1 + 127 - 7, 1), 1, 254)
    scaled = (w * np.exp2(127.0 - byte)[:, None, :]).reshape(k, n).astype(np.float32)
    words = np.ascontiguousarray(scaled.reshape(k // 512, 128, 4, n).transpose(0, 1, 3, 2)).astype(ml_dtypes.float8_e4m3fn).view(np.uint8)
    return words, np.ascontiguousarray(byte.astype(np.uint8).reshape(k // 512, 16, n))


def unpack_weight(words, scales):
    g, p, n, _ = words.shape
    vals = np.ascontiguousarray(words).view(ml_dtypes.float8_e4m3fn).astype(np.float64) * np.repeat(np.exp2(scales.astype(np.float64) - 127.0), 8, axis=1)[..., None]
    return vals.transpose(0, 1, 3, 2).reshape(g * 512, n)


K, T, S, G, H, C = 512, 1024, 512, 2048, 512, 512


def setup_inputs():
    n = np.random.standard_normal
    s = mx_kscale(K)[:, None]
    packed_xT = pack_weight(n((K, T)) * s)
    packed_dT = pack_weight(n((K, G)) / s)
    return {
        "x_words": packed_xT[0],
        "x_scales": packed_xT[1],
        "d_words": packed_dT[0],
        "d_scales": packed_dT[1],
        "gs": (np.random.uniform(0.5, 1.5, (K, 1)) / s).astype(np.float32),
        "offs": striped(np.random.permutation(T)[:S]),
        "k1": striped8(np.random.randint(0, G, (8, H))),
        "n1": striped8(np.stack([np.random.permutation(S) for _ in range(8)])),
        "n2": striped8(np.stack([np.random.permutation(S) for _ in range(8)])),
        "n3": striped8(np.stack([np.random.permutation(S) for _ in range(8)])),
        "cand": striped(np.random.permutation(T)[:C]),
        "two": striped(np.random.permutation(T)[:S]),
        "k2": striped8(np.random.randint(0, G, (8, H))),
        "n4": striped(np.random.permutation(S)),
        "n5": striped(np.random.permutation(S)),
    }


def reference(x_words, x_scales, d_words, d_scales, gs, offs, k1, n1, n2, n3, cand, two, k2, n4, n5):
    x_cand = unpack_weight(x_words, x_scales)[:, unstriped(cand)]
    d_k1 = unpack_weight(d_words, d_scales)[np.arange(K)[:, None], runs(k1, K)]
    xq = unpack_weight(x_words, x_scales)[:, unstriped(offs)]
    h = 0.0625 * (d_k1.T @ xq)
    st = h - (h[np.arange(H)[:, None], runs(n1, H)])
    su = np.maximum(st, st[np.arange(H)[:, None], runs(n2, H)])
    z = f64(gs) * (su + 0.5 * (su[np.arange(H)[:, None], runs(n3, H)]))
    a = 0.0625 * ((x_cand.T @ mxq(z, 0, "e4m3")))
    d_k2 = unpack_weight(d_words, d_scales)[np.arange(K)[:, None], runs(k2, K)]
    x_two = unpack_weight(x_words, x_scales)[:, unstriped(two)]
    b = 0.0625 * (d_k2.T @ x_two)
    return np.maximum(a, b[:, unstriped(n5)]) - (np.minimum(a[:, unstriped(n4)], b))

@@ -1,0 +1,185 @@
+from contextlib import ExitStack
+
+import concourse.mybir as mybir
+
+F32 = mybir.dt.float32
+BF16 = mybir.dt.bfloat16
+I32 = mybir.dt.int32
+U32 = mybir.dt.uint32
+U16 = mybir.dt.uint16
+U8 = mybir.dt.uint8
+FP8X4 = mybir.dt.float8_e4m3fn_x4
+ALU = mybir.AluOpType
+COPY = mybir.ActivationFunctionType.Copy
+
+P = 128
+T, G, S = 1024, 2048, 512
+PACK = 4
+TILES = 4
+HALF = S // 2
+SIXTEENTH = 0.0625
+WIDE = 2 * S
+NARROW = 704
+FLOPS = 3 * 2 * 512 * 512 * 512
+
+
+def tile_picked_pqcjmaxbthree_none_p_kernel(
+    tc, x_words, x_scales, d_words, d_scales, gs, offs, k1, n1, n2, n3, cand, two, k2, n4, n5, out
+):
+    nc = tc.nc
+    with ExitStack() as ctx:
+        keep = ctx.enter_context(tc.tile_pool(name="keep", bufs=1))
+        psum = ctx.enter_context(tc.psum_pool(name="psum", bufs=1))
+
+        def load_list(name, src):
+            tile = keep.tile([P, S // 16], U16, name=name)
+            nc.sync.dma_start(tile[:], src)
+            return tile
+
+        def sb(name, shape, dtype):
+            return keep.tile(shape, dtype, name=name, align_bytes=64)
+
+        xw = sb("xw", [P, T], U32)
+        dw = sb("dw", [P, G], U32)
+        xs = sb("xs", [P, T], U8)
+        ds = sb("ds", [P, G], U8)
+        k1_plane = sb("k1_plane", [P, S], U8)
+        k2_plane = sb("k2_plane", [P, S], U8)
+        nc.gpsimd.memset(ds[:].bitcast(I32), 0)
+        nc.vector.memset(xs[:].bitcast(I32), 0)
+        nc.gpsimd.memset(k1_plane[:].bitcast(I32), 0)
+        nc.gpsimd.memset(k2_plane[:].bitcast(I32), 0)
+
+        k1_l = load_list("k1_l", k1)
+        nc.sync.dma_start(ds[:].bitcast(I32)[0:P:8, :], d_scales[0].bitcast(I32))
+        offs_l = load_list("offs_l", offs)
+        for q in range(4):
+            nc.sync.dma_start(xs[:].bitcast(I32)[32 * q : 32 * q + 4, :], x_scales[0, 4 * q : 4 * q + 4, :].bitcast(I32))
+        nc.sync.dma_start(xw[:].bitcast(I32), x_words[0].rearrange("p n t -> p (n t)").bitcast(I32))
+        nc.sync.dma_start(dw[:].bitcast(I32), d_words[0].rearrange("p n t -> p (n t)").bitcast(I32))
+        n1_l = load_list("n1_l", n1)
+        k2_l = load_list("k2_l", k2)
+        two_l = load_list("two_l", two)
+        n2_l = load_list("n2_l", n2)
+        n3_l = load_list("n3_l", n3)
+        n5_l = load_list("n5_l", n5)
+        cand_l = load_list("cand_l", cand)
+        n4_l = load_list("n4_l", n4)
+        gs4 = sb("gs4", [P, PACK], F32)
+        nc.sync.dma_start(gs4[:], gs.rearrange("(p t) o -> p (t o)", t=PACK))
+
+        h_win = [sb("h_win%d" % t, [P, S], F32) for t in range(TILES)]
+        st_win = [sb("st_win%d" % t, [P, WIDE], F32) for t in range(TILES)]
+        su_win = [sb("su_win%d" % t, [P, WIDE], F32) for t in range(TILES)]
+        b_win = [sb("b_win%d" % t, [P, S], F32) for t in range(TILES)]
+        a_win = [sb("a_win%d" % t, [P, S], F32) for t in range(TILES)]
+
+        def pick(name, table, lst, dtype):
+            tile = sb(name, [P, S], dtype)
+            nc.vector.tensor_copy(tile[:], table[:].indirect(lst[:]))
+            return tile
+
+        def deal(name, src, dtype):
+            tile = sb(name, [P, S], dtype)
+            nc.vector.tensor_copy(
+                tile[:].rearrange("p (t m) -> p m t", t=PACK), src[:].rearrange("p (m t) -> p m t", t=PACK)
+            )
+            return tile
+
+        def place(queue, plane, src):
+            for q in range(4):
+                queue.dma_start(
+                    plane[:].bitcast(I32)[32 * q : 32 * q + 4, :], src[:].bitcast(I32)[32 * q : 32 * q + 32 : 8, :]
+                )
+
+        def product(acc, lhs_w, lhs_s, t, rhs_w, rhs_s):
+            rows = slice(P * t, P * (t + 1))
+            nc.tensor.matmul_mx(
+                out=acc, lhsT=lhs_w[:, rows].bitcast(FP8X4), lhsT_scale=lhs_s[:, rows],
+                rhs=rhs_w.bitcast(FP8X4), rhs_scale=rhs_s, start=True, stop=True,
+            )
+
+        def fetch(on_scalar, dst, win, lst):
+            if on_scalar:
+                nc.scalar.activation(dst, win[:].indirect(lst), COPY)
+            else:
+                nc.vector.tensor_copy(dst, win[:].indirect(lst))
+
+        def fetch_half(on_scalar, dst, win, lst, u):
+            fetch(on_scalar, dst[:, HALF * u : HALF * (u + 1)], win, lst[:, HALF // 16 * u : HALF // 16 * (u + 1)])
+
+        place(nc.scalar, k1_plane, deal("k1_s_dealt", pick("k1_s", ds, k1_l, U8), U8))
+        xq_s = pick("xq_s", xs, offs_l, U8)
+        xq_w = pick("xq_w", xw, offs_l, U32)
+        k1_w = deal("k1_w_dealt", pick("k1_w", dw, k1_l, U32), U32)
+
+        h_ps = [psum.tile([P, S], F32, name="h_ps%d" % t, tag="ha%d" % t) for t in range(TILES)]
+        for t in range(TILES):
+            product(h_ps[t][:], k1_w, k1_plane, t, xq_w[:], xq_s[:])
+
+        place(nc.sync, k2_plane, pick("k2_s", ds, k2_l, U8))
+        two_s = pick("two_s", xs, two_l, U8)
+        two_w = pick("two_w", xw, two_l, U32)
+        k2_w = pick("k2_w", dw, k2_l, U32)
+
+        for t in range(TILES):
+            nc.scalar.activation(h_win[t][:, :S], h_ps[t][:], COPY, scale=SIXTEENTH)
+            for u in range(2):
+                fetch_half(True, st_win[t][:, S:], h_win[t], n1_l, u)
+            nc.vector.scalar_tensor_tensor(
+                st_win[t][:, :S], h_ps[t][:], SIXTEENTH, st_win[t][:, S:], ALU.mult, ALU.subtract
+            )
+        for t in range(TILES):
+            fetch(True, su_win[t][:, S:], st_win[t], n2_l[:])
+            nc.vector.tensor_tensor(su_win[t][:, :S], st_win[t][:, :S], su_win[t][:, S:], ALU.max)
+
+        b_ps = [psum.tile([P, S], F32, name="b_ps%d" % t) for t in range(TILES)]
+        for t in range(TILES):
+            product(b_ps[t][:], k2_w, k2_plane, t, two_w[:], two_s[:])
+
+        cand_s = pick("cand_s", xs, cand_l, U8)
+        cand_w = pick("cand_w", xw, cand_l, U32)
+
+        su_n3 = sb("su_n3", [P, TILES, S], F32)
+        w = [sb("w%d" % u, [P, TILES, HALF], F32) for u in range(2)]
+        z_bf = [sb("z_bf%d" % u, [P, HALF * PACK], BF16) for u in range(2)]
+        z_w = sb("z_w", [P, S], U32)
+        z_s = sb("z_s", [P, S], U8)
+        a_ps = [psum.tile([P, S], F32, name="a_ps%d" % t, tag="ha%d" % t) for t in range(TILES)]
+        for u in range(2):
+            cols = slice(HALF * u, HALF * (u + 1))
+            for t in range(TILES):
+                fetch_half(t >= 2, su_n3[:, t, :], su_win[t], n3_l, u)
+                nc.vector.scalar_tensor_tensor(
+                    w[u][:, t, :], su_n3[:, t, cols], 0.5, su_win[t][:, cols], ALU.mult, ALU.add
+                )
+            nc.vector.tensor_tensor(
+                z_bf[u][:].rearrange("p (c i t) -> p c t i", i=4, t=PACK),
+                w[u][:].rearrange("p t (c i) -> p c t i", i=4),
+                gs4[:].unsqueeze(1).unsqueeze(3).broadcast_to([P, HALF // 4, PACK, 4]),
+                ALU.mult,
+            )
+            nc.vector.quantize_mx(out=z_w[:, cols].bitcast(FP8X4), scales=z_s[:, cols], in_=z_bf[u][:])
+            for t in range(TILES):
+                product(a_ps[t][:, cols], cand_w, cand_s, t, z_w[:, cols], z_s[:, cols])
+
+        b_n5 = [sb("b_n5_%d" % t, [P, S], F32) for t in range(TILES)]
+        for t in range(TILES):
+            nc.scalar.activation(b_win[t][:], b_ps[t][:], COPY, scale=SIXTEENTH)
+            for u in range(2):
+                fetch_half(t != 2, b_n5[t][:], b_win[t], n5_l, u)
+
+        for t in range(TILES):
+            a_n4 = sb("a_n4_%d" % t, [P, S], F32)
+            hi = sb("hi%d" % t, [P, S], F32)
+            lo = sb("lo%d" % t, [P, S], F32)
+            res = sb("res%d" % t, [P, S], F32)
+            nc.scalar.activation(a_win[t][:], a_ps[t][:], COPY, scale=SIXTEENTH)
+            for u in range(2):
+                fetch_half(True, a_n4[:], a_win[t], n4_l, u)
+            nc.vector.tensor_tensor(hi[:], a_win[t][:], b_n5[t][:], ALU.max)
+            pieces = [slice(0, HALF), slice(HALF, S)] if t == TILES - 1 else [slice(0, S)]
+            for cols in pieces:
+                nc.vector.tensor_tensor(lo[:, cols], a_n4[:, cols], b_win[t][:, cols], ALU.min)
+                nc.vector.tensor_tensor(res[:, cols], hi[:, cols], lo[:, cols], ALU.subtract)
+                nc.sync.dma_start(out[P * t : P * (t + 1), cols], res[:, cols])

@@ -16,11 +16,27 @@ P = 128
 T, G, S = 1024, 2048, 512
 PACK = 4
 TILES = 4
+LAST = TILES - 1
 HALF = S // 2
+QUADRANTS = 4
+ENTRIES = 16
 SIXTEENTH = 0.0625
-WIDE = 2 * S
-NARROW = 704
 FLOPS = 3 * 2 * 512 * 512 * 512
+
+VECTOR_TILE_N2 = 2
+VECTOR_TILE_N3 = 3
+VECTOR_TILE_B = 2
+VECTOR_TILE_A = 0
+PLANES_BY_DMA = 2
+GPSIMD_TILES_OUT = 2
+
+WORD_BYTES = 4 * S
+K2_WORDS_AT = 0
+K1_WORDS_AT = WORD_BYTES - 64
+K2_SCALES_AT = WORD_BYTES
+TWO_SCALES_AT = K2_SCALES_AT + S
+CAND_SCALES_AT = TWO_SCALES_AT + S
+TWO_WORDS_AT = K1_WORDS_AT + WORD_BYTES - 64
 
 
 def tile_picked_pqcjmaxbthree_none_p_kernel(
@@ -29,15 +45,19 @@ def tile_picked_pqcjmaxbthree_none_p_kernel(
     nc = tc.nc
     with ExitStack() as ctx:
         keep = ctx.enter_context(tc.tile_pool(name="keep", bufs=1))
+        staging = ctx.enter_context(tc.tile_pool(name="staging", bufs=1))
         psum = ctx.enter_context(tc.psum_pool(name="psum", bufs=1))
 
         def load_list(name, src):
-            tile = keep.tile([P, S // 16], U16, name=name)
+            tile = keep.tile([P, S // ENTRIES], U16, name=name)
             nc.sync.dma_start(tile[:], src)
             return tile
 
-        def sb(name, shape, dtype):
-            return keep.tile(shape, dtype, name=name, align_bytes=64)
+        def sb(name, shape, dtype, tag=None):
+            return keep.tile(shape, dtype, name=name, tag=tag or name, align_bytes=64)
+
+        def entries(lst, cols):
+            return lst[:, cols.start // ENTRIES : cols.stop // ENTRIES]
 
         xw = sb("xw", [P, T], U32)
         dw = sb("dw", [P, G], U32)
@@ -45,38 +65,43 @@ def tile_picked_pqcjmaxbthree_none_p_kernel(
         ds = sb("ds", [P, G], U8)
         k1_plane = sb("k1_plane", [P, S], U8)
         k2_plane = sb("k2_plane", [P, S], U8)
+        zeros = sb("zeros", [P, S], F32)
         nc.gpsimd.memset(ds[:].bitcast(I32), 0)
         nc.vector.memset(xs[:].bitcast(I32), 0)
+        nc.vector.memset(zeros[:], 0.0)
         nc.gpsimd.memset(k1_plane[:].bitcast(I32), 0)
         nc.gpsimd.memset(k2_plane[:].bitcast(I32), 0)
 
         k1_l = load_list("k1_l", k1)
         nc.sync.dma_start(ds[:].bitcast(I32)[0:P:8, :], d_scales[0].bitcast(I32))
         offs_l = load_list("offs_l", offs)
-        for q in range(4):
+        for q in range(QUADRANTS):
             nc.sync.dma_start(xs[:].bitcast(I32)[32 * q : 32 * q + 4, :], x_scales[0, 4 * q : 4 * q + 4, :].bitcast(I32))
-        nc.sync.dma_start(xw[:].bitcast(I32), x_words[0].rearrange("p n t -> p (n t)").bitcast(I32))
         nc.sync.dma_start(dw[:].bitcast(I32), d_words[0].rearrange("p n t -> p (n t)").bitcast(I32))
+        nc.sync.dma_start(xw[:].bitcast(I32), x_words[0].rearrange("p n t -> p (n t)").bitcast(I32))
         n1_l = load_list("n1_l", n1)
         k2_l = load_list("k2_l", k2)
         two_l = load_list("two_l", two)
         n2_l = load_list("n2_l", n2)
-        n3_l = load_list("n3_l", n3)
-        n5_l = load_list("n5_l", n5)
         cand_l = load_list("cand_l", cand)
-        n4_l = load_list("n4_l", n4)
         gs4 = sb("gs4", [P, PACK], F32)
         nc.sync.dma_start(gs4[:], gs.rearrange("(p t) o -> p (t o)", t=PACK))
+        n3_l = load_list("n3_l", n3)
+        n5_l = load_list("n5_l", n5)
+        n4_l = load_list("n4_l", n4)
 
-        h_win = [sb("h_win%d" % t, [P, S], F32) for t in range(TILES)]
-        st_win = [sb("st_win%d" % t, [P, WIDE], F32) for t in range(TILES)]
-        su_win = [sb("su_win%d" % t, [P, WIDE], F32) for t in range(TILES)]
-        b_win = [sb("b_win%d" % t, [P, S], F32) for t in range(TILES)]
-        a_win = [sb("a_win%d" % t, [P, S], F32) for t in range(TILES)]
+        h_win = [sb("h_win%d" % t, [P, 2 * S], F32) for t in range(TILES)]
+        st_win = [sb("st_win%d" % t, [P, 2 * S], F32) for t in range(TILES)]
+        su_win = [sb("su_win%d" % t, [P, 2 * S], F32) for t in range(TILES)]
+        for t in range(TILES):
+            nc.scalar.activation(h_win[t][:, S:], zeros[:], COPY)
 
-        def pick(name, table, lst, dtype):
-            tile = sb(name, [P, S], dtype)
-            nc.vector.tensor_copy(tile[:], table[:].indirect(lst[:]))
+        def gather_packed(dst, table, offsets):
+            nc.vector.tensor_copy(dst, table[:].indirect(offsets))
+
+        def pick_staged(name, table, lst, dtype, at):
+            tile = staging.tile([P, S], dtype, name=name, align_bytes=64, offset=at)
+            gather_packed(tile[:], table, lst[:])
             return tile
 
         def deal(name, src, dtype):
@@ -87,7 +112,7 @@ def tile_picked_pqcjmaxbthree_none_p_kernel(
             return tile
 
         def place(queue, plane, src):
-            for q in range(4):
+            for q in range(QUADRANTS):
                 queue.dma_start(
                     plane[:].bitcast(I32)[32 * q : 32 * q + 4, :], src[:].bitcast(I32)[32 * q : 32 * q + 32 : 8, :]
                 )
@@ -99,87 +124,109 @@ def tile_picked_pqcjmaxbthree_none_p_kernel(
                 rhs=rhs_w.bitcast(FP8X4), rhs_scale=rhs_s, start=True, stop=True,
             )
 
-        def fetch(on_scalar, dst, win, lst):
-            if on_scalar:
-                nc.scalar.activation(dst, win[:].indirect(lst), COPY)
+        def look_up(on_vector, dst, win, offsets):
+            if on_vector:
+                nc.vector.tensor_copy(dst, win[:].indirect(offsets))
             else:
-                nc.vector.tensor_copy(dst, win[:].indirect(lst))
+                nc.scalar.activation(dst, win[:].indirect(offsets), COPY)
 
-        def fetch_half(on_scalar, dst, win, lst, u):
-            fetch(on_scalar, dst[:, HALF * u : HALF * (u + 1)], win, lst[:, HALF // 16 * u : HALF // 16 * (u + 1)])
+        def leave_psum(on_vector, dst, acc):
+            if on_vector:
+                nc.vector.tensor_scalar_mul(dst, acc, SIXTEENTH)
+            else:
+                nc.scalar.activation(dst, acc, COPY, scale=SIXTEENTH)
 
-        place(nc.scalar, k1_plane, deal("k1_s_dealt", pick("k1_s", ds, k1_l, U8), U8))
-        xq_s = pick("xq_s", xs, offs_l, U8)
-        xq_w = pick("xq_w", xw, offs_l, U32)
-        k1_w = deal("k1_w_dealt", pick("k1_w", dw, k1_l, U32), U32)
+        halves = [slice(0, HALF), slice(HALF, S)]
+        k1_s = sb("k1_s", [P, S], U8)
+        gather_packed(k1_s[:], ds, k1_l[:])
+        place(nc.scalar, k1_plane, deal("k1_s_dealt", k1_s, U8))
+        xq_s = sb("xq_s", [P, S], U8)
+        xq_w = sb("xq_w", [P, S], U32)
+        gather_packed(xq_s[:, halves[0]], xs, entries(offs_l, halves[0]))
+        k1_picked = pick_staged("k1_w", dw, k1_l, U32, K1_WORDS_AT)
+        gather_packed(xq_s[:, halves[1]], xs, entries(offs_l, halves[1]))
+        k1_w = deal("k1_w_dealt", k1_picked, U32)
+        h_ps = {}
+        for u, cols in enumerate(halves):
+            gather_packed(xq_w[:, cols], xw, entries(offs_l, cols))
+            for t in range(TILES):
+                bank = ("bank_b%d" if u == 0 else "bank_a%d") % t
+                h_ps[t, u] = psum.tile([P, HALF], F32, name="h_ps%d_%d" % (t, u), tag=bank)
+                product(h_ps[t, u][:], k1_w, k1_plane, t, xq_w[:, cols], xq_s[:, cols])
 
-        h_ps = [psum.tile([P, S], F32, name="h_ps%d" % t, tag="ha%d" % t) for t in range(TILES)]
+        place(nc.sync, k2_plane, pick_staged("k2_s", ds, k2_l, U8, K2_SCALES_AT))
+        two_s = pick_staged("two_s", xs, two_l, U8, TWO_SCALES_AT)
+        two_w = pick_staged("two_w", xw, two_l, U32, TWO_WORDS_AT)
+        k2_w = pick_staged("k2_w", dw, k2_l, U32, K2_WORDS_AT)
+
         for t in range(TILES):
-            product(h_ps[t][:], k1_w, k1_plane, t, xq_w[:], xq_s[:])
-
-        place(nc.sync, k2_plane, pick("k2_s", ds, k2_l, U8))
-        two_s = pick("two_s", xs, two_l, U8)
-        two_w = pick("two_w", xw, two_l, U32)
-        k2_w = pick("k2_w", dw, k2_l, U32)
-
+            leave_psum(False, h_win[t][:, halves[0]], h_ps[t, 0][:])
         for t in range(TILES):
-            nc.scalar.activation(h_win[t][:, :S], h_ps[t][:], COPY, scale=SIXTEENTH)
-            for u in range(2):
-                fetch_half(True, st_win[t][:, S:], h_win[t], n1_l, u)
-            nc.vector.scalar_tensor_tensor(
-                st_win[t][:, :S], h_ps[t][:], SIXTEENTH, st_win[t][:, S:], ALU.mult, ALU.subtract
-            )
-        for t in range(TILES):
-            fetch(True, su_win[t][:, S:], st_win[t], n2_l[:])
-            nc.vector.tensor_tensor(su_win[t][:, :S], st_win[t][:, :S], su_win[t][:, S:], ALU.max)
+            leave_psum(False, h_win[t][:, halves[1]], h_ps[t, 1][:])
+            look_up(False, st_win[t][:, S:], h_win[t], n1_l[:])
+            nc.vector.tensor_tensor(st_win[t][:, :S], h_win[t][:, :S], st_win[t][:, S:], ALU.subtract)
 
-        b_ps = [psum.tile([P, S], F32, name="b_ps%d" % t) for t in range(TILES)]
+        b_ps = [psum.tile([P, S], F32, name="b_ps%d" % t, tag="bank_b%d" % t) for t in range(TILES)]
         for t in range(TILES):
             product(b_ps[t][:], k2_w, k2_plane, t, two_w[:], two_s[:])
 
-        cand_s = pick("cand_s", xs, cand_l, U8)
-        cand_w = pick("cand_w", xw, cand_l, U32)
+        cand_s = pick_staged("cand_s", xs, cand_l, U8, CAND_SCALES_AT)
+        cand_w = sb("cand_w", [P, S], U32, tag="xq_w")
+        gather_packed(cand_w[:], xw, cand_l[:])
 
-        su_n3 = sb("su_n3", [P, TILES, S], F32)
-        w = [sb("w%d" % u, [P, TILES, HALF], F32) for u in range(2)]
-        z_bf = [sb("z_bf%d" % u, [P, HALF * PACK], BF16) for u in range(2)]
+        weighted = sb("weighted", [P, TILES, S], F32)
+        for t in range(TILES):
+            st_n2 = sb("st_n2_%d" % t, [P, S], F32)
+            look_up(t == VECTOR_TILE_N2, st_n2[:], st_win[t], n2_l[:])
+            nc.vector.tensor_tensor(su_win[t][:, S:], st_win[t][:, :S], st_n2[:], ALU.max)
+            nc.vector.tensor_scalar_mul(su_win[t][:, :S], su_win[t][:, S:], gs4[:, t : t + 1])
+            if t < PLANES_BY_DMA:
+                nc.sync.dma_start(weighted[:, t, :], su_win[t][:, :S])
+            else:
+                nc.vector.tensor_scalar_mul(weighted[:, t, :], su_win[t][:, S:], gs4[:, t : t + 1])
+
+        half_n3 = sb("half_n3", [P, TILES, S], F32)
         z_w = sb("z_w", [P, S], U32)
         z_s = sb("z_s", [P, S], U8)
-        a_ps = [psum.tile([P, S], F32, name="a_ps%d" % t, tag="ha%d" % t) for t in range(TILES)]
-        for u in range(2):
-            cols = slice(HALF * u, HALF * (u + 1))
-            for t in range(TILES):
-                fetch_half(t >= 2, su_n3[:, t, :], su_win[t], n3_l, u)
-                nc.vector.scalar_tensor_tensor(
-                    w[u][:, t, :], su_n3[:, t, cols], 0.5, su_win[t][:, cols], ALU.mult, ALU.add
-                )
-            nc.vector.tensor_tensor(
-                z_bf[u][:].rearrange("p (c i t) -> p c t i", i=4, t=PACK),
-                w[u][:].rearrange("p t (c i) -> p c t i", i=4),
-                gs4[:].unsqueeze(1).unsqueeze(3).broadcast_to([P, HALF // 4, PACK, 4]),
-                ALU.mult,
-            )
-            nc.vector.quantize_mx(out=z_w[:, cols].bitcast(FP8X4), scales=z_s[:, cols], in_=z_bf[u][:])
-            for t in range(TILES):
-                product(a_ps[t][:, cols], cand_w, cand_s, t, z_w[:, cols], z_s[:, cols])
+        z_bf = sb("z_bf", [P, S * PACK], BF16)
+        for t in range(TILES):
+            looked_up = su_win[t][:].indirect(n3_l[:])
+            if t == VECTOR_TILE_N3:
+                nc.vector.tensor_scalar(half_n3[:, t, :], looked_up, 0.5, 0.0, ALU.mult, ALU.add)
+            else:
+                nc.scalar.activation(half_n3[:, t, :], looked_up, COPY, scale=0.5)
+        nc.vector.tensor_tensor(
+            z_bf[:].rearrange("p (c i t) -> p c t i", i=4, t=PACK),
+            weighted[:].rearrange("p t (c i) -> p c t i", i=4),
+            half_n3[:].rearrange("p t (c i) -> p c t i", i=4),
+            ALU.add,
+        )
+        nc.vector.quantize_mx(out=z_w[:].bitcast(FP8X4), scales=z_s[:], in_=z_bf[:])
+        a_ps = [psum.tile([P, S], F32, name="a_ps%d" % t, tag="bank_a%d" % t) for t in range(TILES)]
+        for t in range(TILES):
+            product(a_ps[t][:], cand_w, cand_s, t, z_w[:], z_s[:])
 
+        b_win = su_win[::-1]
+        a_win = h_win
         b_n5 = [sb("b_n5_%d" % t, [P, S], F32) for t in range(TILES)]
         for t in range(TILES):
-            nc.scalar.activation(b_win[t][:], b_ps[t][:], COPY, scale=SIXTEENTH)
-            for u in range(2):
-                fetch_half(t != 2, b_n5[t][:], b_win[t], n5_l, u)
+            leave_psum(t == VECTOR_TILE_B, b_win[t][:, :S], b_ps[t][:])
+            look_up(t == VECTOR_TILE_B, b_n5[t][:], b_win[t], n5_l[:])
 
         for t in range(TILES):
             a_n4 = sb("a_n4_%d" % t, [P, S], F32)
-            hi = sb("hi%d" % t, [P, S], F32)
-            lo = sb("lo%d" % t, [P, S], F32)
-            res = sb("res%d" % t, [P, S], F32)
-            nc.scalar.activation(a_win[t][:], a_ps[t][:], COPY, scale=SIXTEENTH)
-            for u in range(2):
-                fetch_half(True, a_n4[:], a_win[t], n4_l, u)
-            nc.vector.tensor_tensor(hi[:], a_win[t][:], b_n5[t][:], ALU.max)
-            pieces = [slice(0, HALF), slice(HALF, S)] if t == TILES - 1 else [slice(0, S)]
+            larger = sb("larger%d" % t, [P, S], F32)
+            smaller = sb("smaller%d" % t, [P, S], F32)
+            result = sb("result%d" % t, [P, S], F32)
+            pieces = halves if t == LAST else [slice(0, S)]
+            leave_psum(t == VECTOR_TILE_A, a_win[t][:, :S], a_ps[t][:])
             for cols in pieces:
-                nc.vector.tensor_tensor(lo[:, cols], a_n4[:, cols], b_win[t][:, cols], ALU.min)
-                nc.vector.tensor_tensor(res[:, cols], hi[:, cols], lo[:, cols], ALU.subtract)
-                nc.sync.dma_start(out[P * t : P * (t + 1), cols], res[:, cols])
+                look_up(t == VECTOR_TILE_A, a_n4[:, cols], a_win[t], entries(n4_l, cols))
+            nc.vector.scalar_tensor_tensor(larger[:], a_ps[t][:], SIXTEENTH, b_n5[t][:], ALU.mult, ALU.max)
+            for cols in pieces:
+                nc.vector.scalar_tensor_tensor(
+                    smaller[:, cols], b_ps[t][:, cols], SIXTEENTH, a_n4[:, cols], ALU.mult, ALU.min
+                )
+                engine = nc.gpsimd if t < GPSIMD_TILES_OUT else nc.vector
+                engine.tensor_tensor(result[:, cols], larger[:, cols], smaller[:, cols], ALU.subtract)
+                nc.sync.dma_start(out[P * t : P * (t + 1), cols], result[:, cols])

@@ -23,11 +23,12 @@ ENTRIES = 16
 SIXTEENTH = 0.0625
 FLOPS = 3 * 2 * 512 * 512 * 512
 
-VECTOR_TILE_N2 = 2
-VECTOR_TILE_N3 = 3
+VECTOR_TILE_N2 = 1
+VECTOR_TILE_N3 = 2
 VECTOR_TILE_B = 2
 VECTOR_TILE_A = 0
-PLANES_BY_DMA = 2
+PLANES_BY_DMA = 3
+GPSIMD_TILES_ST = 3
 GPSIMD_TILES_OUT = 2
 
 WORD_BYTES = 4 * S
@@ -164,7 +165,8 @@ def tile_picked_pqcjmaxbthree_none_p_kernel(
         for t in range(TILES):
             leave_psum(False, h_win[t][:, halves[1]], h_ps[t, 1][:])
             look_up(False, st_win[t][:, S:], h_win[t], n1_l[:])
-            nc.vector.tensor_tensor(st_win[t][:, :S], h_win[t][:, :S], st_win[t][:, S:], ALU.subtract)
+            engine = nc.gpsimd if t < GPSIMD_TILES_ST else nc.vector
+            engine.tensor_tensor(st_win[t][:, :S], h_win[t][:, :S], st_win[t][:, S:], ALU.subtract)
 
         b_ps = [psum.tile([P, S], F32, name="b_ps%d" % t, tag="bank_b%d" % t) for t in range(TILES)]
         for t in range(TILES):
@@ -206,7 +208,7 @@ def tile_picked_pqcjmaxbthree_none_p_kernel(
         for t in range(TILES):
             product(a_ps[t][:], cand_w, cand_s, t, z_w[:], z_s[:])
 
-        b_win = su_win[::-1]
+        b_win = su_win
         a_win = h_win
         b_n5 = [sb("b_n5_%d" % t, [P, S], F32) for t in range(TILES)]
         for t in range(TILES):

@@ -198,9 +198,9 @@ def tile_picked_pqcjmaxbthree_none_p_kernel(
             else:
                 nc.scalar.activation(half_n3[:, t, :], looked_up, COPY, scale=0.5)
         nc.vector.tensor_tensor(
-            z_bf[:].rearrange("p (c i t) -> p c t i", i=4, t=PACK),
-            weighted[:].rearrange("p t (c i) -> p c t i", i=4),
-            half_n3[:].rearrange("p t (c i) -> p c t i", i=4),
+            z_bf[:].rearrange("p (c i t) -> p c t i", i=8, t=PACK),
+            weighted[:].rearrange("p t (c i) -> p c t i", i=8),
+            half_n3[:].rearrange("p t (c i) -> p c t i", i=8),
             ALU.add,
         )
         nc.vector.quantize_mx(out=z_w[:].bitcast(FP8X4), scales=z_s[:], in_=z_bf[:])

from contextlib import ExitStack

import concourse.mybir as mybir

F32 = mybir.dt.float32
BF16 = mybir.dt.bfloat16
I32 = mybir.dt.int32
U32 = mybir.dt.uint32
U16 = mybir.dt.uint16
U8 = mybir.dt.uint8
FP8X4 = mybir.dt.float8_e4m3fn_x4
ALU = mybir.AluOpType
COPY = mybir.ActivationFunctionType.Copy

P = 128
T, G, S = 1024, 2048, 512
PACK = 4
TILES = 4
LAST = TILES - 1
HALF = S // 2
QUADRANTS = 4
ENTRIES = 16
SIXTEENTH = 0.0625
FLOPS = 3 * 2 * 512 * 512 * 512

VECTOR_TILE_N2 = 1
VECTOR_TILE_N3 = 2
VECTOR_TILE_B = 2
VECTOR_TILE_A = 0
PLANES_BY_DMA = 3
GPSIMD_TILES_ST = 3
GPSIMD_TILES_OUT = 2

WORD_BYTES = 4 * S
K2_WORDS_AT = 0
K1_WORDS_AT = WORD_BYTES - 64
K2_SCALES_AT = WORD_BYTES
TWO_SCALES_AT = K2_SCALES_AT + S
CAND_SCALES_AT = TWO_SCALES_AT + S
TWO_WORDS_AT = K1_WORDS_AT + WORD_BYTES - 64


def tile_picked_pqcjmaxbthree_none_p_kernel(
    tc, x_words, x_scales, d_words, d_scales, gs, offs, k1, n1, n2, n3, cand, two, k2, n4, n5, out
):
    nc = tc.nc
    with ExitStack() as ctx:
        keep = ctx.enter_context(tc.tile_pool(name="keep", bufs=1))
        staging = ctx.enter_context(tc.tile_pool(name="staging", bufs=1))
        psum = ctx.enter_context(tc.psum_pool(name="psum", bufs=1))

        def load_list(name, src):
            tile = keep.tile([P, S // ENTRIES], U16, name=name)
            nc.sync.dma_start(tile[:], src)
            return tile

        def sb(name, shape, dtype, tag=None):
            return keep.tile(shape, dtype, name=name, tag=tag or name, align_bytes=64)

        def entries(lst, cols):
            return lst[:, cols.start // ENTRIES : cols.stop // ENTRIES]

        xw = sb("xw", [P, T], U32)
        dw = sb("dw", [P, G], U32)
        xs = sb("xs", [P, T], U8)
        ds = sb("ds", [P, G], U8)
        k1_plane = sb("k1_plane", [P, S], U8)
        k2_plane = sb("k2_plane", [P, S], U8)
        zeros = sb("zeros", [P, S], F32)
        nc.gpsimd.memset(ds[:].bitcast(I32), 0)
        nc.vector.memset(xs[:].bitcast(I32), 0)
        nc.vector.memset(zeros[:], 0.0)
        nc.gpsimd.memset(k1_plane[:].bitcast(I32), 0)
        nc.gpsimd.memset(k2_plane[:].bitcast(I32), 0)

        k1_l = load_list("k1_l", k1)
        nc.sync.dma_start(ds[:].bitcast(I32)[0:P:8, :], d_scales[0].bitcast(I32))
        offs_l = load_list("offs_l", offs)
        for q in range(QUADRANTS):
            nc.sync.dma_start(xs[:].bitcast(I32)[32 * q : 32 * q + 4, :], x_scales[0, 4 * q : 4 * q + 4, :].bitcast(I32))
        nc.sync.dma_start(dw[:].bitcast(I32), d_words[0].rearrange("p n t -> p (n t)").bitcast(I32))
        nc.sync.dma_start(xw[:].bitcast(I32), x_words[0].rearrange("p n t -> p (n t)").bitcast(I32))
        n1_l = load_list("n1_l", n1)
        k2_l = load_list("k2_l", k2)
        two_l = load_list("two_l", two)
        n2_l = load_list("n2_l", n2)
        cand_l = load_list("cand_l", cand)
        gs4 = sb("gs4", [P, PACK], F32)
        nc.sync.dma_start(gs4[:], gs.rearrange("(p t) o -> p (t o)", t=PACK))
        n3_l = load_list("n3_l", n3)
        n5_l = load_list("n5_l", n5)
        n4_l = load_list("n4_l", n4)

        h_win = [sb("h_win%d" % t, [P, 2 * S], F32) for t in range(TILES)]
        st_win = [sb("st_win%d" % t, [P, 2 * S], F32) for t in range(TILES)]
        su_win = [sb("su_win%d" % t, [P, 2 * S], F32) for t in range(TILES)]
        for t in range(TILES):
            nc.scalar.activation(h_win[t][:, S:], zeros[:], COPY)

        def gather_packed(dst, table, offsets):
            nc.vector.tensor_copy(dst, table[:].indirect(offsets))

        def pick_staged(name, table, lst, dtype, at):
            tile = staging.tile([P, S], dtype, name=name, align_bytes=64, offset=at)
            gather_packed(tile[:], table, lst[:])
            return tile

        def deal(name, src, dtype):
            tile = sb(name, [P, S], dtype)
            nc.vector.tensor_copy(
                tile[:].rearrange("p (t m) -> p m t", t=PACK), src[:].rearrange("p (m t) -> p m t", t=PACK)
            )
            return tile

        def place(queue, plane, src):
            for q in range(QUADRANTS):
                queue.dma_start(
                    plane[:].bitcast(I32)[32 * q : 32 * q + 4, :], src[:].bitcast(I32)[32 * q : 32 * q + 32 : 8, :]
                )

        def product(acc, lhs_w, lhs_s, t, rhs_w, rhs_s):
            rows = slice(P * t, P * (t + 1))
            nc.tensor.matmul_mx(
                out=acc, lhsT=lhs_w[:, rows].bitcast(FP8X4), lhsT_scale=lhs_s[:, rows],
                rhs=rhs_w.bitcast(FP8X4), rhs_scale=rhs_s, start=True, stop=True,
            )

        def look_up(on_vector, dst, win, offsets):
            if on_vector:
                nc.vector.tensor_copy(dst, win[:].indirect(offsets))
            else:
                nc.scalar.activation(dst, win[:].indirect(offsets), COPY)

        def leave_psum(on_vector, dst, acc):
            if on_vector:
                nc.vector.tensor_scalar_mul(dst, acc, SIXTEENTH)
            else:
                nc.scalar.activation(dst, acc, COPY, scale=SIXTEENTH)

        halves = [slice(0, HALF), slice(HALF, S)]
        k1_s = sb("k1_s", [P, S], U8)
        gather_packed(k1_s[:], ds, k1_l[:])
        place(nc.scalar, k1_plane, deal("k1_s_dealt", k1_s, U8))
        xq_s = sb("xq_s", [P, S], U8)
        xq_w = sb("xq_w", [P, S], U32)
        gather_packed(xq_s[:, halves[0]], xs, entries(offs_l, halves[0]))
        k1_picked = pick_staged("k1_w", dw, k1_l, U32, K1_WORDS_AT)
        gather_packed(xq_s[:, halves[1]], xs, entries(offs_l, halves[1]))
        k1_w = deal("k1_w_dealt", k1_picked, U32)
        h_ps = {}
        for u, cols in enumerate(halves):
            gather_packed(xq_w[:, cols], xw, entries(offs_l, cols))
            for t in range(TILES):
                bank = ("bank_b%d" if u == 0 else "bank_a%d") % t
                h_ps[t, u] = psum.tile([P, HALF], F32, name="h_ps%d_%d" % (t, u), tag=bank)
                product(h_ps[t, u][:], k1_w, k1_plane, t, xq_w[:, cols], xq_s[:, cols])

        place(nc.sync, k2_plane, pick_staged("k2_s", ds, k2_l, U8, K2_SCALES_AT))
        two_s = pick_staged("two_s", xs, two_l, U8, TWO_SCALES_AT)
        two_w = pick_staged("two_w", xw, two_l, U32, TWO_WORDS_AT)
        k2_w = pick_staged("k2_w", dw, k2_l, U32, K2_WORDS_AT)

        for t in range(TILES):
            leave_psum(False, h_win[t][:, halves[0]], h_ps[t, 0][:])
        for t in range(TILES):
            leave_psum(False, h_win[t][:, halves[1]], h_ps[t, 1][:])
            look_up(False, st_win[t][:, S:], h_win[t], n1_l[:])
            engine = nc.gpsimd if t < GPSIMD_TILES_ST else nc.vector
            engine.tensor_tensor(st_win[t][:, :S], h_win[t][:, :S], st_win[t][:, S:], ALU.subtract)

        b_ps = [psum.tile([P, S], F32, name="b_ps%d" % t, tag="bank_b%d" % t) for t in range(TILES)]
        for t in range(TILES):
            product(b_ps[t][:], k2_w, k2_plane, t, two_w[:], two_s[:])

        cand_s = pick_staged("cand_s", xs, cand_l, U8, CAND_SCALES_AT)
        cand_w = sb("cand_w", [P, S], U32, tag="xq_w")
        gather_packed(cand_w[:], xw, cand_l[:])

        weighted = sb("weighted", [P, TILES, S], F32)
        for t in range(TILES):
            st_n2 = sb("st_n2_%d" % t, [P, S], F32)
            look_up(t == VECTOR_TILE_N2, st_n2[:], st_win[t], n2_l[:])
            nc.vector.tensor_tensor(su_win[t][:, S:], st_win[t][:, :S], st_n2[:], ALU.max)
            nc.vector.tensor_scalar_mul(su_win[t][:, :S], su_win[t][:, S:], gs4[:, t : t + 1])
            if t < PLANES_BY_DMA:
                nc.sync.dma_start(weighted[:, t, :], su_win[t][:, :S])
            else:
                nc.vector.tensor_scalar_mul(weighted[:, t, :], su_win[t][:, S:], gs4[:, t : t + 1])

        half_n3 = sb("half_n3", [P, TILES, S], F32)
        z_w = sb("z_w", [P, S], U32)
        z_s = sb("z_s", [P, S], U8)
        z_bf = sb("z_bf", [P, S * PACK], BF16)
        for t in range(TILES):
            looked_up = su_win[t][:].indirect(n3_l[:])
            if t == VECTOR_TILE_N3:
                nc.vector.tensor_scalar(half_n3[:, t, :], looked_up, 0.5, 0.0, ALU.mult, ALU.add)
            else:
                nc.scalar.activation(half_n3[:, t, :], looked_up, COPY, scale=0.5)
        nc.vector.tensor_tensor(
            z_bf[:].rearrange("p (c i t) -> p c t i", i=8, t=PACK),
            weighted[:].rearrange("p t (c i) -> p c t i", i=8),
            half_n3[:].rearrange("p t (c i) -> p c t i", i=8),
            ALU.add,
        )
        nc.vector.quantize_mx(out=z_w[:].bitcast(FP8X4), scales=z_s[:], in_=z_bf[:])
        a_ps = [psum.tile([P, S], F32, name="a_ps%d" % t, tag="bank_a%d" % t) for t in range(TILES)]
        for t in range(TILES):
            product(a_ps[t][:], cand_w, cand_s, t, z_w[:], z_s[:])

        b_win = su_win
        a_win = h_win
        b_n5 = [sb("b_n5_%d" % t, [P, S], F32) for t in range(TILES)]
        for t in range(TILES):
            leave_psum(t == VECTOR_TILE_B, b_win[t][:, :S], b_ps[t][:])
            look_up(t == VECTOR_TILE_B, b_n5[t][:], b_win[t], n5_l[:])

        for t in range(TILES):
            a_n4 = sb("a_n4_%d" % t, [P, S], F32)
            larger = sb("larger%d" % t, [P, S], F32)
            smaller = sb("smaller%d" % t, [P, S], F32)
            result = sb("result%d" % t, [P, S], F32)
            pieces = halves if t == LAST else [slice(0, S)]
            leave_psum(t == VECTOR_TILE_A, a_win[t][:, :S], a_ps[t][:])
            for cols in pieces:
                look_up(t == VECTOR_TILE_A, a_n4[:, cols], a_win[t], entries(n4_l, cols))
            nc.vector.scalar_tensor_tensor(larger[:], a_ps[t][:], SIXTEENTH, b_n5[t][:], ALU.mult, ALU.max)
            for cols in pieces:
                nc.vector.scalar_tensor_tensor(
                    smaller[:, cols], b_ps[t][:, cols], SIXTEENTH, a_n4[:, cols], ALU.mult, ALU.min
                )
                engine = nc.gpsimd if t < GPSIMD_TILES_OUT else nc.vector
                engine.tensor_tensor(result[:, cols], larger[:, cols], smaller[:, cols], ALU.subtract)
                nc.sync.dma_start(out[P * t : P * (t + 1), cols], result[:, cols])
